import numpy as np
CORES = [0,1]
N = 2
def setup_inputs(rng):
    return {"x": rng.standard_normal((N, 128, 8192), dtype=np.float32)}
def reference(x):
    b = 8192 // N
    blocks = x.reshape(N, 128, N, b)
    return {"y": np.ascontiguousarray(blocks.transpose(2, 1, 0, 3)).reshape(N, 128, 8192)}

SCRATCH = {
    "send": ("sbuf", [128, 4096], "float32"),
    "land": ("sbuf", [128, 4096], "float32"),
}
SEMAPHORES = ["loaded", "read", "arrived", "stored"]

ENGINES = 16


def rank_program(g, core, T, topo):
    rank = T.rank_of(core)
    if rank is None:
        return
    n = len(T.cores)
    b = T.x.shape[1] // n
    peer_rank = 1 - rank
    peer = T.cores[peer_rank]
    rid, pid, sengine = topo.addr(peer)

    g.dma_start(T.send[:], T.x[:, peer_rank * b:(peer_rank + 1) * b]).then_inc(T.sem.loaded, 16)
    g.dma_start(T.y[:, rank * b:(rank + 1) * b], T.x[:, rank * b:(rank + 1) * b]).then_inc(T.sem.stored, 16)

    g.wait_ge(T.sem.loaded, 16)
    g.remote_dma(T.land[:], T.send[:], T.sem.arrived, T.sem.read, pid, rid, topo.mask(core, peer))

    g.wait_ge(T.sem.arrived, ENGINES)
    g.dma_start(T.y[:, peer_rank * b:(peer_rank + 1) * b], T.land[:]).then_inc(T.sem.stored, 16)

    g.wait_ge(T.sem.stored, 32)
    g.wait_ge(T.sem.read, ENGINES)
